import numpy as np
import ml_dtypes


def mxq(x, axis, fmt="e4m3"):
    dtype, down = {"e4m3": (ml_dtypes.float8_e4m3fn, 7), "e5m2": (ml_dtypes.float8_e5m2, 14)}[fmt]
    v = np.moveaxis(np.asarray(x, np.float32).astype(ml_dtypes.bfloat16).astype(np.float64), axis, -1)
    blocks = v.reshape(v.shape[:-1] + (-1, 32))
    amax = np.abs(blocks).max(-1, keepdims=True)
    byte = np.maximum(np.where(amax > 0, np.frexp(amax)[1] - 1 + 127, 0) - down, 1)
    scale = np.exp2(byte - 127.0)
    codes = (blocks / scale).astype(np.float32).astype(dtype).astype(np.float64)
    return np.moveaxis((codes * scale).reshape(v.shape), -1, axis)


WIDE = False


def mx_kscale(k):
    if not WIDE:
        return np.ones(k)
    levels = np.array([10, -10, 5, -5, 0])
    if k % 512:
        return np.exp2(np.random.permutation(np.resize(levels, k // 32))).repeat(32)
    a = np.empty((k // 512, 16))
    for p in range(k // 512):
        a[p, :8] = np.random.permutation(np.resize(levels, 8))
        for g in range(8):
            far = levels[np.abs(levels - a[p, g]) >= 10]
            a[p, g + 8] = far[np.random.randint(len(far))]
    return np.exp2(a.ravel()).repeat(32)


def f64(x):
    return np.asarray(x).astype(np.float64)


def striped(idx):
    return np.tile(np.asarray(idx).reshape(-1, 16).T, (8, 1)).astype(np.uint16)


def unstriped(offs):
    return offs[:16].T.reshape(-1).astype(np.int64)


E2M1 = np.array([0.0, 0.5, 1.0, 1.5, 2.0, 3.0, 4.0, 6.0, -0.0, -0.5, -1.0, -1.5, -2.0, -3.0, -4.0, -6.0])


def pack_weight(w, fmt):
    k, n = w.shape
    w = f64(np.asarray(w, np.float32).astype(ml_dtypes.bfloat16)).reshape(k // 32, 32, n)
    amax = np.abs(w).max(1)
    if fmt == "e4m3":
        byte = np.frexp(amax)[1] - 1 + 127 - 7
    else:
        mant, ex = np.frexp(amax / 6.0)
        byte = np.where(mant > 0.5, ex, ex - 1) + 127
    byte = np.clip(np.where(amax > 0, byte, 1), 1, 254)
    scaled = (w * np.exp2(127.0 - byte)[:, None, :]).reshape(k, n).astype(np.float32)
    by_word = np.ascontiguousarray(scaled.reshape(k // 512, 128, 4, n).transpose(0, 1, 3, 2))
    if fmt == "e4m3":
        words = by_word.astype(ml_dtypes.float8_e4m3fn).view(np.uint8)
    else:
        c = by_word.astype(ml_dtypes.float4_e2m1fn).view(np.uint8) & 0xF
        words = (c[..., 0::2] | (c[..., 1::2] << 4)).reshape(k // 512, 128, 2 * n)
    return np.ascontiguousarray(words), np.ascontiguousarray(byte.astype(np.uint8).reshape(k // 512, 16, n))


def unpack_weight(words, scales, fmt):
    g, _, n = scales.shape
    words = np.ascontiguousarray(words).reshape(g, 128, n, -1)
    if fmt == "e4m3":
        vals = words.view(ml_dtypes.float8_e4m3fn).astype(np.float64)
    else:
        nib = np.empty((g, 128, n, 4), np.uint8)
        nib[..., 0::2] = words & 0xF
        nib[..., 1::2] = words >> 4
        vals = E2M1[nib]
    vals = vals * np.repeat(np.exp2(scales.astype(np.float64) - 127.0), 8, axis=1)[..., None]
    return vals.transpose(0, 1, 3, 2).reshape(g * 512, n)


def sigmoid(v):
    return 1.0 / (1.0 + np.exp(-v))


D, T, I, Q, E, M = 512, 2048, 512, 256, 512, 1024


def setup_inputs():
    n = np.random.standard_normal
    idx = np.random.permutation(T)[:I]
    idx2 = np.random.permutation(M)[:Q]
    fd = mx_kscale(D)
    fi = mx_kscale(I)
    ti = np.ones(T)
    ti[idx] = fi
    keysp = pack_weight(n((D, T)) / fd[:, None], "e4m3")
    return {
        "query": (n((D, Q)) * 1.2 / np.sqrt(D) * fd[:, None]).astype(np.float32),
        "keys_words": keysp[0],
        "keys_scales": keysp[1],
        "guess": np.tile(np.random.uniform(0.05, 0.3, T), (128, 1)).astype(np.float32),
        "steep": np.tile(np.random.uniform(1.0, 3.0, T), (128, 1)).astype(np.float32),
        "thr": np.tile(np.random.uniform(-0.5, 1.0, T), (128, 1)).astype(np.float32),
        "lam": (np.random.uniform(0.6, 1.5, (Q, 1))).astype(np.float32),
        "pull": (np.random.uniform(0.3, 0.9, (Q, 1))).astype(np.float32),
        "os": (np.random.uniform(4.0, 16.0, (1, I)) * fi).astype(np.float32),
        "vals": (n((E, T)) / ti).astype(np.float32),
        "old": (n((E, M)) * 2.0).astype(np.float32),
        "fade": (np.random.uniform(0.3, 0.9, (1, M))).astype(np.float32),
        "offs": striped(idx),
        "offs2": striped(idx2),
    }


def reference(query, keys_words, keys_scales, guess, steep, thr, lam, pull, os, vals, old, fade, offs, offs2):
    idx = unstriped(offs)
    idx2 = unstriped(offs2)
    keysu = unpack_weight(keys_words, keys_scales, "e4m3")
    queryq = mxq(f64(query), 0, "e4m3")
    keysidxg = keysu[:, idx]
    a = queryq.T @ keysidxg
    sg = sigmoid((a - f64(thr)[:1][:, idx]) * f64(steep)[:1][:, idx])
    s = np.log(sg * (1.0 - f64(guess)[:1][:, idx]) + f64(guess)[:1][:, idx]) * f64(lam)
    p = np.exp(s - np.max(s, axis=1, keepdims=True))
    r = p / np.sum(p, axis=1, keepdims=True)
    r1 = np.pad(r, ((0, 0), (1, 0)))[:, :I]
    w = r - r1 * f64(pull)
    wo1 = w * f64(os)
    wt1 = wo1.T
    vt1 = f64(vals)[:, idx].T
    vt1q = mxq(vt1, 0, "e4m3")
    wt1q = mxq(wt1, 0, "e4m3")
    o = vt1q.T @ wt1q
    of = np.zeros((E, M))
    of[:, idx2] = o
    y = f64(old) * f64(fade) + of
    return y

@@ -1,0 +1,308 @@
+from contextlib import ExitStack
+
+import concourse.mybir as mybir
+from concourse.masks import make_identity
+
+D, T, I, Q, E, M = 512, 2048, 512, 256, 512, 1024
+FLOPS = 2 * D * Q * I + 2 * I * E * Q
+BYTES = 4 * D * Q + D * T + 16 * T + 3 * 4 * T + 4 * (2 * Q + I + M) + 4 * E * T + 2 * 4 * E * M + 2 * 128 * (I + Q) // 16
+
+F32 = mybir.dt.float32
+BF16 = mybir.dt.bfloat16
+I32 = mybir.dt.int32
+U32 = mybir.dt.uint32
+U16 = mybir.dt.uint16
+U8 = mybir.dt.uint8
+FP8X4 = mybir.dt.float8_e4m3fn_x4
+ALU = mybir.AluOpType
+ACT = mybir.ActivationFunctionType
+
+P = 128
+LAST = P - 1
+PAD = 8
+
+
+def tile_attend_answerodds_stepwise_written_kernel(
+    tc, query, keys_words, keys_scales, guess, steep, thr, lam, pull, slot_gain, vals, old, fade, offs, offs2, out
+):
+    nc = tc.nc
+    with ExitStack() as ctx:
+        lists = ctx.enter_context(tc.tile_pool(name="lists", bufs=1))
+        sb = ctx.enter_context(tc.tile_pool(name="sb", bufs=1))
+        ps = ctx.enter_context(tc.psum_pool(name="ps", bufs=1))
+
+        def bank(letter, shape, name):
+            return ps.tile(shape, F32, name=name, tag="bank" + letter)
+
+        slot_list = lists.tile([P, I // 16], U16, name="slot_list")
+        place_list = lists.tile([P, Q // 16], U16, name="place_list")
+
+        key_bytes = sb.tile([P, T], U8, name="key_bytes", tag="win_d", align_bytes=64)
+        nc.gpsimd.memset(key_bytes[:].bitcast(I32), 0)
+        nc.sync.dma_start(slot_list[:], offs)
+        for quad in range(4):
+            nc.scalar.dma_start(
+                key_bytes[32 * quad : 32 * quad + 4, :].bitcast(I32),
+                keys_scales[0, 4 * quad : 4 * quad + 4, :].bitcast(I32),
+            )
+        steep_win = sb.tile([P, T], F32, name="steep_win", tag="win_a", align_bytes=64)
+        thr_win = sb.tile([P, T], F32, name="thr_win", tag="win_b", align_bytes=64)
+        nc.sync.dma_start(steep_win[LAST:P, :], steep[0:1, :])
+        nc.sync.dma_start(thr_win[LAST:P, :], thr[0:1, :])
+        guess_win = sb.tile([P, T], F32, name="guess_win", tag="win_g", align_bytes=64)
+        nc.sync.dma_start(guess_win[LAST:P, :], guess[0:1, :])
+        nc.sync.dma_start(place_list[:], offs2)
+        fade_rows = sb.tile([P, P], F32, name="fade_rows")
+        nc.sync.dma_start(fade_rows[120:128, :], fade.rearrange("o (j p) -> (o j) p", p=P))
+        q_raw = sb.tile([P, 4, Q], F32, name="q_raw", tag="win_c", align_bytes=64)
+        nc.sync.dma_start(q_raw[:], query.rearrange("(p j) q -> p j q", j=4))
+        key_words = sb.tile([P, T], I32, name="key_words", tag="hold1", align_bytes=64)
+        nc.sync.dma_start(key_words[:], keys_words[0].rearrange("p t r -> p (t r)").bitcast(I32))
+        nc.vector.memset(steep_win[0:LAST, 0 : T - 1], 0.0)
+        nc.vector.memset(steep_win[0:LAST, T - 1 : T], 0.0)
+
+        ident = sb.tile([P, P], F32, name="ident")
+        make_identity(nc, ident[:])
+        nc.gpsimd.memset(thr_win[0:LAST, :], 0.0)
+        nc.gpsimd.memset(guess_win[0:LAST, :], 0.0)
+        nc.gpsimd.memset(fade_rows[0:120, :], 0.0)
+
+        warm = sb.tile([P, 1], F32, name="warm")
+        nc.scalar.activation(warm[:], ident[:, 0:1], ACT.Sigmoid)
+
+        def gather_row(window, name, letter, tag):
+            got = sb.tile([P, I], F32, name=name + "_got", tag=tag, align_bytes=64)
+            nc.vector.tensor_copy(got[:], window[:].indirect(slot_list[:]))
+            turned = bank(letter, [P, 4, P], name + "_turned")
+            for t in range(4):
+                nc.tensor.transpose(turned[:, t, :], got[:, t * P : (t + 1) * P], ident[:])
+            col = sb.tile([P, 4], F32, name=name + "_col", tag=name + "_col")
+            nc.scalar.copy(col[:], turned[:, :, LAST])
+            return col
+
+        steep_col = gather_row(steep_win, "steep", "A", "steep_got")
+        thr_col = gather_row(thr_win, "thr", "B", "thr_got")
+        val_win = []
+
+        def load_values(j, tag):
+            window = sb.tile([P, T], F32, name="val_win%d" % j, tag=tag, align_bytes=64)
+            nc.sync.dma_start(window[:], vals[j * P : (j + 1) * P, :])
+            val_win.append(window)
+
+        load_values(0, "win_a")
+
+        q_bf = sb.tile([P, Q, 4], BF16, name="q_bf", tag="hold0", align_bytes=64)
+        nc.scalar.copy(q_bf[:], q_raw[:].rearrange("p j q -> p q j"))
+        smalls = sb.tile([P, 24], F32, name="smalls", tag="steep_got", align_bytes=64)
+        lam_col, pull_col, gain_col = smalls[:, 0:2], smalls[:, 8:10], smalls[:, 16:20]
+        nc.sync.dma_start(gain_col, slot_gain.rearrange("o (p t) -> p (o t)", t=4))
+        with nc.allow_non_contiguous_dma(reason="one value a partition"):
+            nc.sync.dma_start(lam_col, lam.rearrange("(h p) o -> p (h o)", p=P))
+            nc.sync.dma_start(pull_col, pull.rearrange("(h p) o -> p (h o)", p=P))
+        load_values(1, "win_b")
+        q_codes = sb.tile([P, Q], U32, name="q_codes", tag="hold2", align_bytes=64)
+        q_scales = sb.tile([P, Q], U8, name="q_scales", tag="hold4", align_bytes=64)
+
+        got_bytes = sb.tile([P, I], U8, name="got_bytes", tag="got_bytes", align_bytes=64)
+        nc.vector.tensor_copy(got_bytes[:], key_bytes[:].indirect(slot_list[:]))
+        load_values(2, "win_c")
+        nc.vector.quantize_mx(q_codes[:].bitcast(FP8X4), q_scales[:], q_bf[:].rearrange("p q j -> p (q j)"))
+        sig_bias = sb.tile([P, 4], F32, name="sig_bias", tag="sig_bias", align_bytes=64)
+        nc.vector.scalar_tensor_tensor(sig_bias[:], thr_col[:], -1.0, steep_col[:], ALU.mult, ALU.mult)
+        got_words = sb.tile([P, I], U32, name="got_words", tag="hold3", align_bytes=64)
+        nc.vector.tensor_copy(got_words[:], key_words[:].bitcast(U32).indirect(slot_list[:]))
+
+        load_values(3, "win_d")
+
+        score = [bank("DE"[h], [P, 2, Q], "score%d" % h) for h in range(2)]
+        sig = sb.tile([P, 4, Q], F32, name="sig", tag="sig", align_bytes=64)
+        for t in range(4):
+            nc.tensor.matmul_mx(
+                score[t // 2][:, t % 2, :],
+                lhsT=got_words[:, t * P : (t + 1) * P].bitcast(FP8X4),
+                lhsT_scale=got_bytes[:, t * P : (t + 1) * P],
+                rhs=q_codes[:].bitcast(FP8X4),
+                rhs_scale=q_scales[:],
+                start=True,
+                stop=True,
+            )
+        for t in range(4):
+            nc.scalar.activation(
+                sig[:, t, :], score[t // 2][:, t % 2, :], ACT.Sigmoid,
+                bias=sig_bias[:, t : t + 1], scale=steep_col[:, t : t + 1],
+            )
+
+        guess_col = gather_row(guess_win, "guess", "C", "hold1")
+        miss_col = sb.tile([P, 4], F32, name="miss_col")
+        nc.scalar.activation(miss_col[:], guess_col[:], ACT.Copy, scale=-1.0, bias=1.0)
+
+        places = [sb.tile([P, M], F32, name="places%d" % j, tag="hold%d" % [0, 4, 2, 3][j], align_bytes=64) for j in range(4)]
+        for j in range(4):
+            nc.gpsimd.memset(places[j][:], 0.0)
+
+        neg_lam = sb.tile([P, 2], F32, name="neg_lam", tag="sig_bias", align_bytes=64)
+        neg_pull = sb.tile([P, 2], F32, name="neg_pull", tag="steep_col")
+        nc.gpsimd.tensor_scalar(neg_lam[:], lam_col, -1.0, 0.0, ALU.mult, ALU.add)
+        nc.gpsimd.tensor_scalar(neg_pull[:], pull_col, -1.0, 0.0, ALU.mult, ALU.add)
+
+        logc = sb.tile([P, 4, Q], F32, name="logc")
+        for t in range(4):
+            nc.scalar.activation(
+                logc[:, t, :], sig[:, t, :], ACT.Ln, bias=guess_col[:, t : t + 1], scale=miss_col[:, t : t + 1]
+            )
+
+        old_tags = ["thr_got", "got_bytes", "win_g", "hold1"]
+        old_sb = []
+        for c in range(4):
+            chunk = sb.tile([P, 4, 2 * P], F32, name="old_sb%d" % c, tag=old_tags[c], align_bytes=64)
+            nc.sync.dma_start(chunk[:], old[:, 2 * P * c : 2 * P * (c + 1)].rearrange("(j p) m -> p j m", p=P))
+            old_sb.append(chunk)
+
+        gain_all = bank("D", [P, 4, P], "gain_all")
+        for t in range(4):
+            nc.tensor.transpose(gain_all[:, t, :], gain_col[:, t : t + 1].to_broadcast([P, P]), ident[:])
+
+        v_bf = []
+        v_turned = []
+        v_codes = sb.tile([P, E], U32, name="v_codes", align_bytes=64)
+        v_scales = sb.tile([P, E], U8, name="v_scales", align_bytes=64)
+
+        def turn_pairs(src, letter, name):
+            words = src.bitcast(F32)
+            turned = bank(letter, [P, 2, P], name)
+            for u in range(2):
+                nc.tensor.transpose(turned[:, u, :], words[:, u : I // 2 : 2], ident[:])
+            return turned
+
+        def interleave(dst, turned):
+            nc.scalar.copy(dst.bitcast(F32), turned[:].rearrange("p u c -> p c u"))
+
+        def gather_values(j):
+            got = sb.tile([P, I], BF16, name="val_got%d" % j, tag=["val_got0", "val_got1", "sig_bias", "step1"][j], align_bytes=64)
+            nc.vector.tensor_copy(got[:], val_win[j][:].indirect(slot_list[:]))
+            v_turned.append(turn_pairs(got[:], "ABCA"[j], "val_turned%d" % j))
+
+        def group_values(j, tag):
+            grouped = sb.tile([P, P, 4], BF16, name="v_bf%d" % j, tag=tag, align_bytes=64)
+            interleave(grouped[:], v_turned[j])
+            v_bf.append(grouped)
+
+        def quantize_values(j):
+            nc.vector.quantize_mx(
+                v_codes[:, j * P : (j + 1) * P].bitcast(FP8X4),
+                v_scales[:, j * P : (j + 1) * P],
+                v_bf[j][:].rearrange("p c t -> p (c t)"),
+            )
+
+        gather_values(0)
+        gather_values(1)
+
+        log_turned = [bank("FG"[h], [P, 4, P], "log_turned%d" % h) for h in range(2)]
+        for h in range(2):
+            for t in range(4):
+                nc.tensor.transpose(log_turned[h][:, t, :], logc[:, t, h * P : (h + 1) * P], ident[:])
+        neg_s = [sb.tile([P, I], F32, name="neg_s%d" % h, tag=["win_b", "neg_s1"][h], align_bytes=64) for h in range(2)]
+        neg_max = [sb.tile([P, 1], F32, name="neg_max%d" % h, tag="neg_max%d" % h, align_bytes=64) for h in range(2)]
+        for h in range(2):
+            nc.vector.tensor_scalar(
+                neg_s[h][:], log_turned[h][:].rearrange("p t c -> p (t c)"), neg_lam[:, h : h + 1], None,
+                ALU.mult, ALU.min, accum_out=neg_max[h][:],
+            )
+        gather_values(2)
+        prob = [sb.tile([P, PAD + I], F32, name="prob%d" % h) for h in range(2)]
+        total = [sb.tile([P, 1], F32, name="total%d" % h) for h in range(2)]
+        for h in range(2):
+            nc.gpsimd.memset(prob[h][:, PAD - 1 : PAD], 0.0)
+            nc.scalar.activation(
+                prob[h][:, PAD:], neg_s[h][:], ACT.Exp, bias=neg_max[h][:], scale=-1.0, accum_out=total[h][:]
+            )
+        group_values(0, "win_b")
+        group_values(1, "neg_s1")
+        group_values(2, "neg_max1")
+        w_codes = []
+        w_scales = []
+        w_bf = []
+        for h in range(2):
+            step = sb.tile([P, I], F32, name="step%d" % h, tag=["win_c", "step1"][h], align_bytes=64)
+            nc.vector.scalar_tensor_tensor(
+                step[:], prob[h][:, PAD - 1 : PAD - 1 + I], neg_pull[:, h : h + 1], prob[h][:, PAD:],
+                ALU.mult, ALU.add,
+            )
+            inv = sb.tile([P, 1], F32, name="inv%d" % h)
+            nc.vector.reciprocal(inv[:], total[h][:])
+            weight = sb.tile([P, I], BF16, name="weight%d" % h)
+            nc.vector.scalar_tensor_tensor(
+                weight[:].rearrange("q (p t) -> q p t", t=4), step[:].rearrange("q (p t) -> q p t", t=4), inv[:],
+                gain_all[:].rearrange("q t p -> q p t"), ALU.mult, ALU.mult,
+            )
+            grouped = sb.tile([P, P, 4], BF16, name="w_bf%d" % h, align_bytes=64)
+            interleave(grouped[:], turn_pairs(weight[:], "HE"[h], "w_turned%d" % h))
+            w_bf.append(grouped)
+
+        def product(h):
+            codes = sb.tile([P, P], U32, name="w_codes%d" % h, align_bytes=64)
+            scales = sb.tile([P, P], U8, name="w_scales%d" % h, align_bytes=64)
+            nc.vector.quantize_mx(codes[:].bitcast(FP8X4), scales[:], w_bf[h][:].rearrange("p c t -> p (c t)"))
+            w_codes.append(codes)
+            w_scales.append(scales)
+
+        o_sb = [[sb.tile([P, P], F32, name="o_sb%d_%d" % (h, j)) for j in range(4)] for h in range(2)]
+
+        def multiply(h, js, letter):
+            acc = bank(letter, [P, len(js), P], "o_acc%d_%d" % (h, js[0]))
+            for n, j in enumerate(js):
+                nc.tensor.matmul_mx(
+                    acc[:, n, :],
+                    lhsT=v_codes[:, j * P : (j + 1) * P].bitcast(FP8X4),
+                    lhsT_scale=v_scales[:, j * P : (j + 1) * P],
+                    rhs=w_codes[h][:].bitcast(FP8X4),
+                    rhs_scale=w_scales[h][:],
+                    start=True,
+                    stop=True,
+                )
+            for n, j in enumerate(js):
+                nc.scalar.copy(o_sb[h][j][:], acc[:, n, :])
+
+        def scatter(h, j):
+            nc.vector.tensor_copy(places[j][:].indirect(place_list[:, 8 * h : 8 * h + 8]), o_sb[h][j][:])
+
+        product(0)
+        for j in range(3):
+            quantize_values(j)
+        multiply(0, [0, 1, 2], "G")
+        gather_values(3)
+        group_values(3, "v_bf3")
+        product(1)
+        multiply(1, [0, 1, 2], "F")
+
+        quantize_values(3)
+        multiply(0, [3], "H")
+        multiply(1, [3], "E")
+
+        fade_turned = bank("B", [P, P], "fade_turned")
+        nc.tensor.transpose(fade_turned[:], fade_rows[:], ident[:])
+        fade_col = sb.tile([P, 8], F32, name="fade_col")
+        nc.scalar.copy(fade_col[:], fade_turned[:, 120:128])
+        faded = [sb.tile([P, E], F32, name="faded%d" % b) for b in range(8)]
+        for b in range(8):
+            turned = bank("GFHE"[b % 4], [P, 4, P], "old_turned%d" % b)
+            for j in range(4):
+                nc.tensor.transpose(turned[:, j, :], old_sb[b // 2][:, j, (b % 2) * P : (b % 2 + 1) * P], ident[:])
+            nc.scalar.activation(
+                faded[b][:], turned[:].rearrange("p j c -> p (j c)"), ACT.Copy, scale=fade_col[:, b : b + 1]
+            )
+
+        scatter(0, 0)
+        scatter(0, 1)
+        scatter(0, 2)
+        scatter(0, 3)
+        for j in range(4):
+            scatter(1, j)
+            result = sb.tile([P, M], F32, name="result%d" % j)
+            for half in range(2):
+                back = bank("BDCAGFHE"[2 * j + half], [P, 4, P], "back%d_%d" % (j, half))
+                for n in range(4):
+                    nc.tensor.transpose(back[:, n, :], faded[4 * half + n][:, j * P : (j + 1) * P], ident[:])
+                cut = slice(half * 512, (half + 1) * 512)
+                nc.vector.tensor_tensor(result[:, cut], back[:].rearrange("p n c -> p (n c)"), places[j][:, cut], ALU.add)
+            nc.sync.dma_start(out[j * P : (j + 1) * P, :], result[:])

@@ -20,6 +20,7 @@ ACT = mybir.ActivationFunctionType
 P = 128
 LAST = P - 1
 PAD = 8
+HALF = M // 2
 
 
 def tile_attend_answerodds_stepwise_written_kernel(
@@ -34,88 +35,95 @@ def tile_attend_answerodds_stepwise_written_kernel(
         def bank(letter, shape, name):
             return ps.tile(shape, F32, name=name, tag="bank" + letter)
 
+        def tile(shape, dtype, name, after=None):
+            return sb.tile(shape, dtype, name=name, tag=after or name, align_bytes=64)
+
         slot_list = lists.tile([P, I // 16], U16, name="slot_list")
         place_list = lists.tile([P, Q // 16], U16, name="place_list")
 
-        key_bytes = sb.tile([P, T], U8, name="key_bytes", tag="win_d", align_bytes=64)
-        nc.gpsimd.memset(key_bytes[:].bitcast(I32), 0)
+        key_bytes = tile([P, T], U8, "key_bytes")
+        nc.gpsimd.memset(key_bytes[:, 0 : T // 2].bitcast(I32), 0)
+        nc.vector.memset(key_bytes[:, T // 2 : T].bitcast(I32), 0)
         nc.sync.dma_start(slot_list[:], offs)
+        steep_win = tile([P, T], F32, "steep_win")
+        thr_win = tile([P, T], F32, "thr_win")
+        guess_win = tile([P, T], F32, "guess_win")
+        nc.sync.dma_start(steep_win[LAST:P, :], steep[0:1, :])
+        nc.sync.dma_start(thr_win[LAST:P, :], thr[0:1, :])
+        nc.sync.dma_start(guess_win[LAST:P, :], guess[0:1, :])
+        fade_col = tile([P, 8], F32, "fade_col")
+        nc.sync.dma_start(fade_col[:], fade.rearrange("o (p j) -> p (o j)", j=8))
+        gain_col = tile([P, 4], F32, "gain_col")
+        nc.sync.dma_start(gain_col[:], slot_gain.rearrange("o (p t) -> p (o t)", t=4))
+        q_raw = tile([P, 4, Q], F32, "q_raw")
+        nc.sync.dma_start(q_raw[:], query.rearrange("(p j) q -> p j q", j=4))
+        key_words = tile([P, T], I32, "key_words")
+        nc.sync.dma_start(key_words[:], keys_words[0].rearrange("p t r -> p (t r)").bitcast(I32))
         for quad in range(4):
-            nc.scalar.dma_start(
+            nc.sync.dma_start(
                 key_bytes[32 * quad : 32 * quad + 4, :].bitcast(I32),
                 keys_scales[0, 4 * quad : 4 * quad + 4, :].bitcast(I32),
             )
-        steep_win = sb.tile([P, T], F32, name="steep_win", tag="win_a", align_bytes=64)
-        thr_win = sb.tile([P, T], F32, name="thr_win", tag="win_b", align_bytes=64)
-        nc.sync.dma_start(steep_win[LAST:P, :], steep[0:1, :])
-        nc.sync.dma_start(thr_win[LAST:P, :], thr[0:1, :])
-        guess_win = sb.tile([P, T], F32, name="guess_win", tag="win_g", align_bytes=64)
-        nc.sync.dma_start(guess_win[LAST:P, :], guess[0:1, :])
         nc.sync.dma_start(place_list[:], offs2)
-        fade_rows = sb.tile([P, P], F32, name="fade_rows")
-        nc.sync.dma_start(fade_rows[120:128, :], fade.rearrange("o (j p) -> (o j) p", p=P))
-        q_raw = sb.tile([P, 4, Q], F32, name="q_raw", tag="win_c", align_bytes=64)
-        nc.sync.dma_start(q_raw[:], query.rearrange("(p j) q -> p j q", j=4))
-        key_words = sb.tile([P, T], I32, name="key_words", tag="hold1", align_bytes=64)
-        nc.sync.dma_start(key_words[:], keys_words[0].rearrange("p t r -> p (t r)").bitcast(I32))
+        val_win = [tile([P, T], F32, "val_win%d" % j) for j in range(4)]
+        old_rows = [tile([P, M], F32, "old_rows%d" % j) for j in range(4)]
+        row_factors = tile([P, 2, 8], F32, "row_factors")
+        for j in range(2):
+            nc.sync.dma_start(val_win[j][:], vals[j * P : (j + 1) * P, :])
+        with nc.allow_non_contiguous_dma(reason="one value a partition"):
+            nc.sync.dma_start(row_factors[:, 0, 0:2], lam.rearrange("(h p) o -> p (h o)", p=P))
+            nc.sync.dma_start(row_factors[:, 1, 0:2], pull.rearrange("(h p) o -> p (h o)", p=P))
+        for j in range(2, 4):
+            nc.sync.dma_start(val_win[j][:], vals[j * P : (j + 1) * P, :])
+        for j in range(4):
+            nc.sync.dma_start(old_rows[j][:], old[j * P : (j + 1) * P, :])
+
         nc.vector.memset(steep_win[0:LAST, 0 : T - 1], 0.0)
         nc.vector.memset(steep_win[0:LAST, T - 1 : T], 0.0)
 
-        ident = sb.tile([P, P], F32, name="ident")
+        ident = tile([P, P], F32, "ident")
         make_identity(nc, ident[:])
         nc.gpsimd.memset(thr_win[0:LAST, :], 0.0)
         nc.gpsimd.memset(guess_win[0:LAST, :], 0.0)
-        nc.gpsimd.memset(fade_rows[0:120, :], 0.0)
 
-        warm = sb.tile([P, 1], F32, name="warm")
+        warm = tile([P, 1], F32, "warm")
         nc.scalar.activation(warm[:], ident[:, 0:1], ACT.Sigmoid)
 
-        def gather_row(window, name, letter, tag):
-            got = sb.tile([P, I], F32, name=name + "_got", tag=tag, align_bytes=64)
+        def gather_row(window, name, letter, after=None):
+            got = tile([P, I], F32, name + "_got", after)
             nc.vector.tensor_copy(got[:], window[:].indirect(slot_list[:]))
             turned = bank(letter, [P, 4, P], name + "_turned")
             for t in range(4):
                 nc.tensor.transpose(turned[:, t, :], got[:, t * P : (t + 1) * P], ident[:])
-            col = sb.tile([P, 4], F32, name=name + "_col", tag=name + "_col")
+            col = tile([P, 4], F32, name + "_col")
             nc.scalar.copy(col[:], turned[:, :, LAST])
             return col
 
-        steep_col = gather_row(steep_win, "steep", "A", "steep_got")
-        thr_col = gather_row(thr_win, "thr", "B", "thr_got")
-        val_win = []
+        steep_col = gather_row(steep_win, "steep", "A")
+        thr_col = gather_row(thr_win, "thr", "B")
 
-        def load_values(j, tag):
-            window = sb.tile([P, T], F32, name="val_win%d" % j, tag=tag, align_bytes=64)
-            nc.sync.dma_start(window[:], vals[j * P : (j + 1) * P, :])
-            val_win.append(window)
-
-        load_values(0, "win_a")
-
-        q_bf = sb.tile([P, Q, 4], BF16, name="q_bf", tag="hold0", align_bytes=64)
+        q_bf = tile([P, Q, 4], BF16, "q_bf")
         nc.scalar.copy(q_bf[:], q_raw[:].rearrange("p j q -> p q j"))
-        smalls = sb.tile([P, 24], F32, name="smalls", tag="steep_got", align_bytes=64)
-        lam_col, pull_col, gain_col = smalls[:, 0:2], smalls[:, 8:10], smalls[:, 16:20]
-        nc.sync.dma_start(gain_col, slot_gain.rearrange("o (p t) -> p (o t)", t=4))
-        with nc.allow_non_contiguous_dma(reason="one value a partition"):
-            nc.sync.dma_start(lam_col, lam.rearrange("(h p) o -> p (h o)", p=P))
-            nc.sync.dma_start(pull_col, pull.rearrange("(h p) o -> p (h o)", p=P))
-        load_values(1, "win_b")
-        q_codes = sb.tile([P, Q], U32, name="q_codes", tag="hold2", align_bytes=64)
-        q_scales = sb.tile([P, Q], U8, name="q_scales", tag="hold4", align_bytes=64)
-
-        got_bytes = sb.tile([P, I], U8, name="got_bytes", tag="got_bytes", align_bytes=64)
+        q_codes = tile([P, Q], U32, "q_codes")
+        q_scales = tile([P, Q], U8, "q_scales")
+        got_bytes = tile([P, I], U8, "got_bytes")
         nc.vector.tensor_copy(got_bytes[:], key_bytes[:].indirect(slot_list[:]))
-        load_values(2, "win_c")
         nc.vector.quantize_mx(q_codes[:].bitcast(FP8X4), q_scales[:], q_bf[:].rearrange("p q j -> p (q j)"))
-        sig_bias = sb.tile([P, 4], F32, name="sig_bias", tag="sig_bias", align_bytes=64)
+        sig_bias = tile([P, 4], F32, "sig_bias")
         nc.vector.scalar_tensor_tensor(sig_bias[:], thr_col[:], -1.0, steep_col[:], ALU.mult, ALU.mult)
-        got_words = sb.tile([P, I], U32, name="got_words", tag="hold3", align_bytes=64)
+        got_words = tile([P, I], U32, "got_words")
         nc.vector.tensor_copy(got_words[:], key_words[:].bitcast(U32).indirect(slot_list[:]))
 
-        load_values(3, "win_d")
+        fade_all = tile([P, P, 8], F32, "fade_all")
+        for half in range(2):
+            spread = bank("FG"[half], [P, 4, P], "fade_spread%d" % half)
+            for n in range(4):
+                col = 4 * half + n
+                nc.tensor.transpose(spread[:, n, :], fade_col[:, col : col + 1].to_broadcast([P, P]), ident[:])
+            nc.scalar.copy(fade_all[:, :, 4 * half : 4 * half + 4], spread[:].rearrange("c n p -> c p n"))
 
         score = [bank("DE"[h], [P, 2, Q], "score%d" % h) for h in range(2)]
-        sig = sb.tile([P, 4, Q], F32, name="sig", tag="sig", align_bytes=64)
+        sig = tile([P, 4, Q], F32, "sig")
         for t in range(4):
             nc.tensor.matmul_mx(
                 score[t // 2][:, t % 2, :],
@@ -132,177 +140,127 @@ def tile_attend_answerodds_stepwise_written_kernel(
                 bias=sig_bias[:, t : t + 1], scale=steep_col[:, t : t + 1],
             )
 
-        guess_col = gather_row(guess_win, "guess", "C", "hold1")
-        miss_col = sb.tile([P, 4], F32, name="miss_col")
+        guess_col = gather_row(guess_win, "guess", "C", "key_words")
+        miss_col = tile([P, 4], F32, "miss_col")
         nc.scalar.activation(miss_col[:], guess_col[:], ACT.Copy, scale=-1.0, bias=1.0)
 
-        places = [sb.tile([P, M], F32, name="places%d" % j, tag="hold%d" % [0, 4, 2, 3][j], align_bytes=64) for j in range(4)]
+        places = [tile([P, M], F32, "places%d" % j, ["q_bf", "thr_col", "got_words", "q_codes"][j]) for j in range(4)]
         for j in range(4):
             nc.gpsimd.memset(places[j][:], 0.0)
+        negated = tile([P, 2, 2], F32, "negated", "sig_bias")
+        nc.vector.tensor_scalar(negated[:], row_factors[:, :, 0:2], -1.0, None, ALU.mult)
+        neg_lam, neg_pull = negated[:, 0, :], negated[:, 1, :]
+        prob = [tile([P, PAD + I], F32, "prob%d" % h) for h in range(2)]
+        for h in range(2):
+            nc.gpsimd.memset(prob[h][:, PAD - 1 : PAD], 0.0)
+        fade_flat = fade_all[:].rearrange("c p j -> c (p j)")
+        kept = {}
 
-        neg_lam = sb.tile([P, 2], F32, name="neg_lam", tag="sig_bias", align_bytes=64)
-        neg_pull = sb.tile([P, 2], F32, name="neg_pull", tag="steep_col")
-        nc.gpsimd.tensor_scalar(neg_lam[:], lam_col, -1.0, 0.0, ALU.mult, ALU.add)
-        nc.gpsimd.tensor_scalar(neg_pull[:], pull_col, -1.0, 0.0, ALU.mult, ALU.add)
+        def fade_old(j, engine, after=None):
+            kept[j] = tile([P, M], F32, "kept%d" % j, after)
+            for half in range(2):
+                cut = slice(half * HALF, (half + 1) * HALF)
+                engine.tensor_tensor(kept[j][:, cut], old_rows[j][:, cut], fade_flat[:, cut], ALU.mult)
 
-        logc = sb.tile([P, 4, Q], F32, name="logc")
+        fade_old(0, nc.gpsimd)
+
+        logc = tile([P, 4, Q], F32, "logc")
         for t in range(4):
             nc.scalar.activation(
                 logc[:, t, :], sig[:, t, :], ACT.Ln, bias=guess_col[:, t : t + 1], scale=miss_col[:, t : t + 1]
             )
 
-        old_tags = ["thr_got", "got_bytes", "win_g", "hold1"]
-        old_sb = []
-        for c in range(4):
-            chunk = sb.tile([P, 4, 2 * P], F32, name="old_sb%d" % c, tag=old_tags[c], align_bytes=64)
-            nc.sync.dma_start(chunk[:], old[:, 2 * P * c : 2 * P * (c + 1)].rearrange("(j p) m -> p j m", p=P))
-            old_sb.append(chunk)
-
-        gain_all = bank("D", [P, 4, P], "gain_all")
+        gain_all = bank("H", [P, 4, P], "gain_all")
         for t in range(4):
             nc.tensor.transpose(gain_all[:, t, :], gain_col[:, t : t + 1].to_broadcast([P, P]), ident[:])
 
-        v_bf = []
         v_turned = []
-        v_codes = sb.tile([P, E], U32, name="v_codes", align_bytes=64)
-        v_scales = sb.tile([P, E], U8, name="v_scales", align_bytes=64)
+        v_codes = tile([P, E], U32, "v_codes")
+        v_scales = tile([P, E], U8, "v_scales")
 
         def turn_pairs(src, letter, name):
             words = src.bitcast(F32)
             turned = bank(letter, [P, 2, P], name)
             for u in range(2):
                 nc.tensor.transpose(turned[:, u, :], words[:, u : I // 2 : 2], ident[:])
-            return turned
+            return turned[:].rearrange("p u c -> p c u")
 
-        def interleave(dst, turned):
-            nc.scalar.copy(dst.bitcast(F32), turned[:].rearrange("p u c -> p c u"))
-
-        def gather_values(j):
-            got = sb.tile([P, I], BF16, name="val_got%d" % j, tag=["val_got0", "val_got1", "sig_bias", "step1"][j], align_bytes=64)
+        def gather_values(j, letter, after=None):
+            got = tile([P, I], BF16, "val_got%d" % j, after)
             nc.vector.tensor_copy(got[:], val_win[j][:].indirect(slot_list[:]))
-            v_turned.append(turn_pairs(got[:], "ABCA"[j], "val_turned%d" % j))
+            v_turned.append(turn_pairs(got[:], letter, "val_turned%d" % j))
 
-        def group_values(j, tag):
-            grouped = sb.tile([P, P, 4], BF16, name="v_bf%d" % j, tag=tag, align_bytes=64)
-            interleave(grouped[:], v_turned[j])
-            v_bf.append(grouped)
-
-        def quantize_values(j):
-            nc.vector.quantize_mx(
-                v_codes[:, j * P : (j + 1) * P].bitcast(FP8X4),
-                v_scales[:, j * P : (j + 1) * P],
-                v_bf[j][:].rearrange("p c t -> p (c t)"),
-            )
-
-        gather_values(0)
-        gather_values(1)
+        for j in range(3):
+            gather_values(j, "ABC"[j])
 
         log_turned = [bank("FG"[h], [P, 4, P], "log_turned%d" % h) for h in range(2)]
         for h in range(2):
             for t in range(4):
                 nc.tensor.transpose(log_turned[h][:, t, :], logc[:, t, h * P : (h + 1) * P], ident[:])
-        neg_s = [sb.tile([P, I], F32, name="neg_s%d" % h, tag=["win_b", "neg_s1"][h], align_bytes=64) for h in range(2)]
-        neg_max = [sb.tile([P, 1], F32, name="neg_max%d" % h, tag="neg_max%d" % h, align_bytes=64) for h in range(2)]
+        neg_s = [tile([P, I], F32, "neg_s%d" % h, ["val_win2", None][h]) for h in range(2)]
+        neg_max = [tile([P, 1], F32, "neg_max%d" % h) for h in range(2)]
         for h in range(2):
             nc.vector.tensor_scalar(
                 neg_s[h][:], log_turned[h][:].rearrange("p t c -> p (t c)"), neg_lam[:, h : h + 1], None,
                 ALU.mult, ALU.min, accum_out=neg_max[h][:],
             )
-        gather_values(2)
-        prob = [sb.tile([P, PAD + I], F32, name="prob%d" % h) for h in range(2)]
-        total = [sb.tile([P, 1], F32, name="total%d" % h) for h in range(2)]
+        gather_values(3, "D", "logc")
+        total = [tile([P, 1], F32, "total%d" % h) for h in range(2)]
         for h in range(2):
-            nc.gpsimd.memset(prob[h][:, PAD - 1 : PAD], 0.0)
             nc.scalar.activation(
                 prob[h][:, PAD:], neg_s[h][:], ACT.Exp, bias=neg_max[h][:], scale=-1.0, accum_out=total[h][:]
             )
-        group_values(0, "win_b")
-        group_values(1, "neg_s1")
-        group_values(2, "neg_max1")
-        w_codes = []
-        w_scales = []
+        v_bf = tile([P, 4, P, 4], BF16, "v_bf", "neg_s1")
+        for j in range(4):
+            nc.scalar.copy(v_bf[:, j, :, :].bitcast(F32), v_turned[j])
         w_bf = []
         for h in range(2):
-            step = sb.tile([P, I], F32, name="step%d" % h, tag=["win_c", "step1"][h], align_bytes=64)
+            step = tile([P, I], F32, "step%d" % h, ["val_win3", "logc"][h])
             nc.vector.scalar_tensor_tensor(
                 step[:], prob[h][:, PAD - 1 : PAD - 1 + I], neg_pull[:, h : h + 1], prob[h][:, PAD:],
                 ALU.mult, ALU.add,
             )
-            inv = sb.tile([P, 1], F32, name="inv%d" % h)
+            inv = tile([P, 1], F32, "inv%d" % h)
             nc.vector.reciprocal(inv[:], total[h][:])
-            weight = sb.tile([P, I], BF16, name="weight%d" % h)
+            weight = tile([P, I], BF16, "weight%d" % h)
             nc.vector.scalar_tensor_tensor(
                 weight[:].rearrange("q (p t) -> q p t", t=4), step[:].rearrange("q (p t) -> q p t", t=4), inv[:],
                 gain_all[:].rearrange("q t p -> q p t"), ALU.mult, ALU.mult,
             )
-            grouped = sb.tile([P, P, 4], BF16, name="w_bf%d" % h, align_bytes=64)
-            interleave(grouped[:], turn_pairs(weight[:], "HE"[h], "w_turned%d" % h))
+            grouped = tile([P, P, 4], BF16, "w_bf%d" % h)
+            nc.scalar.copy(grouped[:].bitcast(F32), turn_pairs(weight[:], "FG"[h], "w_turned%d" % h))
             w_bf.append(grouped)
 
-        def product(h):
-            codes = sb.tile([P, P], U32, name="w_codes%d" % h, align_bytes=64)
-            scales = sb.tile([P, P], U8, name="w_scales%d" % h, align_bytes=64)
-            nc.vector.quantize_mx(codes[:].bitcast(FP8X4), scales[:], w_bf[h][:].rearrange("p c t -> p (c t)"))
-            w_codes.append(codes)
-            w_scales.append(scales)
-
-        o_sb = [[sb.tile([P, P], F32, name="o_sb%d_%d" % (h, j)) for j in range(4)] for h in range(2)]
-
-        def multiply(h, js, letter):
-            acc = bank(letter, [P, len(js), P], "o_acc%d_%d" % (h, js[0]))
-            for n, j in enumerate(js):
-                nc.tensor.matmul_mx(
-                    acc[:, n, :],
-                    lhsT=v_codes[:, j * P : (j + 1) * P].bitcast(FP8X4),
-                    lhsT_scale=v_scales[:, j * P : (j + 1) * P],
-                    rhs=w_codes[h][:].bitcast(FP8X4),
-                    rhs_scale=w_scales[h][:],
-                    start=True,
-                    stop=True,
-                )
-            for n, j in enumerate(js):
-                nc.scalar.copy(o_sb[h][j][:], acc[:, n, :])
-
-        def scatter(h, j):
-            nc.vector.tensor_copy(places[j][:].indirect(place_list[:, 8 * h : 8 * h + 8]), o_sb[h][j][:])
-
-        product(0)
-        for j in range(3):
-            quantize_values(j)
-        multiply(0, [0, 1, 2], "G")
-        gather_values(3)
-        group_values(3, "v_bf3")
-        product(1)
-        multiply(1, [0, 1, 2], "F")
-
-        quantize_values(3)
-        multiply(0, [3], "H")
-        multiply(1, [3], "E")
-
-        fade_turned = bank("B", [P, P], "fade_turned")
-        nc.tensor.transpose(fade_turned[:], fade_rows[:], ident[:])
-        fade_col = sb.tile([P, 8], F32, name="fade_col")
-        nc.scalar.copy(fade_col[:], fade_turned[:, 120:128])
-        faded = [sb.tile([P, E], F32, name="faded%d" % b) for b in range(8)]
-        for b in range(8):
-            turned = bank("GFHE"[b % 4], [P, 4, P], "old_turned%d" % b)
-            for j in range(4):
-                nc.tensor.transpose(turned[:, j, :], old_sb[b // 2][:, j, (b % 2) * P : (b % 2 + 1) * P], ident[:])
-            nc.scalar.activation(
-                faded[b][:], turned[:].rearrange("p j c -> p (j c)"), ACT.Copy, scale=fade_col[:, b : b + 1]
+        nc.vector.quantize_mx(v_codes[:].bitcast(FP8X4), v_scales[:], v_bf[:].rearrange("p j c t -> p (j c t)"))
+        w_codes = tile([P, Q], U32, "w_codes")
+        w_scales = tile([P, Q], U8, "w_scales")
+        for h in range(2):
+            nc.vector.quantize_mx(
+                w_codes[:, h * P : (h + 1) * P].bitcast(FP8X4),
+                w_scales[:, h * P : (h + 1) * P],
+                w_bf[h][:].rearrange("p c t -> p (c t)"),
             )
+        fade_old(2, nc.vector, "logc")
+        fade_old(3, nc.vector, "w_bf1")
+        fade_old(1, nc.gpsimd, "old_rows3")
 
-        scatter(0, 0)
-        scatter(0, 1)
-        scatter(0, 2)
-        scatter(0, 3)
         for j in range(4):
-            scatter(1, j)
-            result = sb.tile([P, M], F32, name="result%d" % j)
+            acc = bank("EABC"[j], [P, Q], "acc%d" % j)
+            nc.tensor.matmul_mx(
+                acc[:],
+                lhsT=v_codes[:, j * P : (j + 1) * P].bitcast(FP8X4),
+                lhsT_scale=v_scales[:, j * P : (j + 1) * P],
+                rhs=w_codes[:].bitcast(FP8X4),
+                rhs_scale=w_scales[:],
+                start=True,
+                stop=True,
+            )
+            mixed = tile([P, Q], F32, "mixed%d" % j)
+            nc.scalar.copy(mixed[:], acc[:])
+            window = places[j]
+            nc.vector.tensor_copy(window[:].indirect(place_list[:]), mixed[:])
+            adder = nc.gpsimd if j < 2 else nc.vector
             for half in range(2):
-                back = bank("BDCAGFHE"[2 * j + half], [P, 4, P], "back%d_%d" % (j, half))
-                for n in range(4):
-                    nc.tensor.transpose(back[:, n, :], faded[4 * half + n][:, j * P : (j + 1) * P], ident[:])
-                cut = slice(half * 512, (half + 1) * 512)
-                nc.vector.tensor_tensor(result[:, cut], back[:].rearrange("p n c -> p (n c)"), places[j][:, cut], ALU.add)
-            nc.sync.dma_start(out[j * P : (j + 1) * P, :], result[:])
+                cut = slice(half * HALF, (half + 1) * HALF)
+                adder.tensor_tensor(kept[j][:, cut], kept[j][:, cut], window[:, cut], ALU.add)
+                nc.sync.dma_start(out[j * P : (j + 1) * P, cut], kept[j][:, cut])

@@ -51,10 +51,9 @@ def tile_attend_answerodds_stepwise_written_kernel(
         nc.sync.dma_start(steep_win[LAST:P, :], steep[0:1, :])
         nc.sync.dma_start(thr_win[LAST:P, :], thr[0:1, :])
         nc.sync.dma_start(guess_win[LAST:P, :], guess[0:1, :])
-        fade_col = tile([P, 8], F32, "fade_col")
-        nc.sync.dma_start(fade_col[:], fade.rearrange("o (p j) -> p (o j)", j=8))
-        gain_col = tile([P, 4], F32, "gain_col")
-        nc.sync.dma_start(gain_col[:], slot_gain.rearrange("o (p t) -> p (o t)", t=4))
+        rows = tile([P, P], F32, "rows")
+        nc.sync.dma_start(rows[112:120, :], fade.rearrange("o (j p) -> (o j) p", p=P))
+        nc.sync.dma_start(rows[120:124, :], slot_gain.rearrange("o (j p) -> (o j) p", p=P))
         q_raw = tile([P, 4, Q], F32, "q_raw")
         nc.sync.dma_start(q_raw[:], query.rearrange("(p j) q -> p j q", j=4))
         key_words = tile([P, T], I32, "key_words")
@@ -64,16 +63,13 @@ def tile_attend_answerodds_stepwise_written_kernel(
                 key_bytes[32 * quad : 32 * quad + 4, :].bitcast(I32),
                 keys_scales[0, 4 * quad : 4 * quad + 4, :].bitcast(I32),
             )
-        nc.sync.dma_start(place_list[:], offs2)
+        nc.sync.dma_start(rows[124:126, :], lam.rearrange("(j p) o -> j (p o)", p=P))
+        nc.sync.dma_start(rows[126:128, :], pull.rearrange("(j p) o -> j (p o)", p=P))
         val_win = [tile([P, T], F32, "val_win%d" % j) for j in range(4)]
         old_rows = [tile([P, M], F32, "old_rows%d" % j) for j in range(4)]
-        row_factors = tile([P, 2, 8], F32, "row_factors")
-        for j in range(2):
-            nc.sync.dma_start(val_win[j][:], vals[j * P : (j + 1) * P, :])
-        with nc.allow_non_contiguous_dma(reason="one value a partition"):
-            nc.sync.dma_start(row_factors[:, 0, 0:2], lam.rearrange("(h p) o -> p (h o)", p=P))
-            nc.sync.dma_start(row_factors[:, 1, 0:2], pull.rearrange("(h p) o -> p (h o)", p=P))
-        for j in range(2, 4):
+        nc.sync.dma_start(val_win[0][:], vals[0:P, :])
+        nc.sync.dma_start(place_list[:], offs2)
+        for j in range(1, 4):
             nc.sync.dma_start(val_win[j][:], vals[j * P : (j + 1) * P, :])
         for j in range(4):
             nc.sync.dma_start(old_rows[j][:], old[j * P : (j + 1) * P, :])
@@ -83,11 +79,9 @@ def tile_attend_answerodds_stepwise_written_kernel(
 
         ident = tile([P, P], F32, "ident")
         make_identity(nc, ident[:])
+        nc.gpsimd.memset(rows[0:112, :], 0.0)
         nc.gpsimd.memset(thr_win[0:LAST, :], 0.0)
         nc.gpsimd.memset(guess_win[0:LAST, :], 0.0)
-
-        warm = tile([P, 1], F32, "warm")
-        nc.scalar.activation(warm[:], ident[:, 0:1], ACT.Sigmoid)
 
         def gather_row(window, name, letter, after=None):
             got = tile([P, I], F32, name + "_got", after)
@@ -109,18 +103,18 @@ def tile_attend_answerodds_stepwise_written_kernel(
         got_bytes = tile([P, I], U8, "got_bytes")
         nc.vector.tensor_copy(got_bytes[:], key_bytes[:].indirect(slot_list[:]))
         nc.vector.quantize_mx(q_codes[:].bitcast(FP8X4), q_scales[:], q_bf[:].rearrange("p q j -> p (q j)"))
-        sig_bias = tile([P, 4], F32, "sig_bias")
-        nc.vector.scalar_tensor_tensor(sig_bias[:], thr_col[:], -1.0, steep_col[:], ALU.mult, ALU.mult)
         got_words = tile([P, I], U32, "got_words")
         nc.vector.tensor_copy(got_words[:], key_words[:].bitcast(U32).indirect(slot_list[:]))
+        sig_bias = tile([P, 4], F32, "sig_bias")
+        nc.vector.scalar_tensor_tensor(sig_bias[:], thr_col[:], -1.0, steep_col[:], ALU.mult, ALU.mult)
 
-        fade_all = tile([P, P, 8], F32, "fade_all")
-        for half in range(2):
-            spread = bank("FG"[half], [P, 4, P], "fade_spread%d" % half)
-            for n in range(4):
-                col = 4 * half + n
-                nc.tensor.transpose(spread[:, n, :], fade_col[:, col : col + 1].to_broadcast([P, P]), ident[:])
-            nc.scalar.copy(fade_all[:, :, 4 * half : 4 * half + 4], spread[:].rearrange("c n p -> c p n"))
+        rows_turned = bank("B", [P, P], "rows_turned")
+        nc.tensor.transpose(rows_turned[:], rows[:], ident[:])
+        cols = tile([P, 16], F32, "cols")
+        nc.scalar.copy(cols[:], rows_turned[:, 112:128])
+        gain_all = bank("H", [P, 4, P], "gain_all")
+        for t in range(4):
+            nc.tensor.transpose(gain_all[:, t, :], cols[:, 8 + t : 9 + t].to_broadcast([P, P]), ident[:])
 
         score = [bank("DE"[h], [P, 2, Q], "score%d" % h) for h in range(2)]
         sig = tile([P, 4, Q], F32, "sig")
@@ -147,32 +141,18 @@ def tile_attend_answerodds_stepwise_written_kernel(
         places = [tile([P, M], F32, "places%d" % j, ["q_bf", "thr_col", "got_words", "q_codes"][j]) for j in range(4)]
         for j in range(4):
             nc.gpsimd.memset(places[j][:], 0.0)
-        negated = tile([P, 2, 2], F32, "negated", "sig_bias")
-        nc.vector.tensor_scalar(negated[:], row_factors[:, :, 0:2], -1.0, None, ALU.mult)
-        neg_lam, neg_pull = negated[:, 0, :], negated[:, 1, :]
+        negated = tile([P, 4], F32, "negated", "sig_bias")
+        nc.vector.tensor_scalar(negated[:], cols[:, 12:16], -1.0, None, ALU.mult)
+        neg_lam, neg_pull = negated[:, 0:2], negated[:, 2:4]
         prob = [tile([P, PAD + I], F32, "prob%d" % h) for h in range(2)]
         for h in range(2):
             nc.gpsimd.memset(prob[h][:, PAD - 1 : PAD], 0.0)
-        fade_flat = fade_all[:].rearrange("c p j -> c (p j)")
-        kept = {}
-
-        def fade_old(j, engine, after=None):
-            kept[j] = tile([P, M], F32, "kept%d" % j, after)
-            for half in range(2):
-                cut = slice(half * HALF, (half + 1) * HALF)
-                engine.tensor_tensor(kept[j][:, cut], old_rows[j][:, cut], fade_flat[:, cut], ALU.mult)
-
-        fade_old(0, nc.gpsimd)
 
         logc = tile([P, 4, Q], F32, "logc")
         for t in range(4):
             nc.scalar.activation(
                 logc[:, t, :], sig[:, t, :], ACT.Ln, bias=guess_col[:, t : t + 1], scale=miss_col[:, t : t + 1]
             )
-
-        gain_all = bank("H", [P, 4, P], "gain_all")
-        for t in range(4):
-            nc.tensor.transpose(gain_all[:, t, :], gain_col[:, t : t + 1].to_broadcast([P, P]), ident[:])
 
         v_turned = []
         v_codes = tile([P, E], U32, "v_codes")
@@ -224,8 +204,7 @@ def tile_attend_answerodds_stepwise_written_kernel(
             nc.vector.reciprocal(inv[:], total[h][:])
             weight = tile([P, I], BF16, "weight%d" % h)
             nc.vector.scalar_tensor_tensor(
-                weight[:].rearrange("q (p t) -> q p t", t=4), step[:].rearrange("q (p t) -> q p t", t=4), inv[:],
-                gain_all[:].rearrange("q t p -> q p t"), ALU.mult, ALU.mult,
+                weight[:], step[:], inv[:], gain_all[:].rearrange("q t p -> q (t p)"), ALU.mult, ALU.mult
             )
             grouped = tile([P, P, 4], BF16, "w_bf%d" % h)
             nc.scalar.copy(grouped[:].bitcast(F32), turn_pairs(weight[:], "FG"[h], "w_turned%d" % h))
@@ -240,9 +219,6 @@ def tile_attend_answerodds_stepwise_written_kernel(
                 w_scales[:, h * P : (h + 1) * P],
                 w_bf[h][:].rearrange("p c t -> p (c t)"),
             )
-        fade_old(2, nc.vector, "logc")
-        fade_old(3, nc.vector, "w_bf1")
-        fade_old(1, nc.gpsimd, "old_rows3")
 
         for j in range(4):
             acc = bank("EABC"[j], [P, Q], "acc%d" % j)
@@ -257,10 +233,24 @@ def tile_attend_answerodds_stepwise_written_kernel(
             )
             mixed = tile([P, Q], F32, "mixed%d" % j)
             nc.scalar.copy(mixed[:], acc[:])
-            window = places[j]
-            nc.vector.tensor_copy(window[:].indirect(place_list[:]), mixed[:])
-            adder = nc.gpsimd if j < 2 else nc.vector
-            for half in range(2):
-                cut = slice(half * HALF, (half + 1) * HALF)
-                adder.tensor_tensor(kept[j][:, cut], kept[j][:, cut], window[:, cut], ALU.add)
-                nc.sync.dma_start(out[j * P : (j + 1) * P, cut], kept[j][:, cut])
+            nc.vector.tensor_copy(places[j][:].indirect(place_list[:]), mixed[:])
+
+        faded = []
+        for b in range(8):
+            turned = bank("EABC"[b % 4], [P, 4, P], "old_turned%d" % b)
+            for j in range(4):
+                nc.tensor.transpose(turned[:, j, :], old_rows[j][:, b * P : (b + 1) * P], ident[:])
+            scaled = tile([P, E], F32, "faded%d" % b)
+            nc.scalar.activation(
+                scaled[:], turned[:].rearrange("p j c -> p (j c)"), ACT.Copy, scale=cols[:, b : b + 1]
+            )
+            faded.append(scaled)
+        for half in range(2):
+            cut = slice(half * HALF, (half + 1) * HALF)
+            for j in range(4):
+                back = bank(["DFGH", "EABC"][half][j], [P, 4, P], "back%d_%d" % (j, half))
+                for n in range(4):
+                    nc.tensor.transpose(back[:, n, :], faded[4 * half + n][:, j * P : (j + 1) * P], ident[:])
+                result = tile([P, HALF], F32, "result%d_%d" % (j, half))
+                nc.vector.tensor_tensor(result[:], back[:].rearrange("p n c -> p (n c)"), places[j][:, cut], ALU.add)
+                nc.sync.dma_start(out[j * P : (j + 1) * P, cut], result[:])

@@ -42,46 +42,34 @@ def tile_attend_answerodds_stepwise_written_kernel(
         place_list = lists.tile([P, Q // 16], U16, name="place_list")
 
         key_bytes = tile([P, T], U8, "key_bytes")
-        nc.gpsimd.memset(key_bytes[:, 0 : T // 2].bitcast(I32), 0)
-        nc.vector.memset(key_bytes[:, T // 2 : T].bitcast(I32), 0)
+        nc.gpsimd.memset(key_bytes[:].bitcast(I32), 0)
         nc.sync.dma_start(slot_list[:], offs)
+        for quad in range(4):
+            nc.scalar.dma_start(
+                key_bytes[32 * quad : 32 * quad + 4, :].bitcast(I32),
+                keys_scales[0, 4 * quad : 4 * quad + 4, :].bitcast(I32),
+            )
         steep_win = tile([P, T], F32, "steep_win")
         thr_win = tile([P, T], F32, "thr_win")
         guess_win = tile([P, T], F32, "guess_win")
         nc.sync.dma_start(steep_win[LAST:P, :], steep[0:1, :])
         nc.sync.dma_start(thr_win[LAST:P, :], thr[0:1, :])
         nc.sync.dma_start(guess_win[LAST:P, :], guess[0:1, :])
-        rows = tile([P, P], F32, "rows")
-        nc.sync.dma_start(rows[112:120, :], fade.rearrange("o (j p) -> (o j) p", p=P))
-        nc.sync.dma_start(rows[120:124, :], slot_gain.rearrange("o (j p) -> (o j) p", p=P))
-        q_raw = tile([P, 4, Q], F32, "q_raw")
-        nc.sync.dma_start(q_raw[:], query.rearrange("(p j) q -> p j q", j=4))
+        nc.sync.dma_start(place_list[:], offs2)
         key_words = tile([P, T], I32, "key_words")
         nc.sync.dma_start(key_words[:], keys_words[0].rearrange("p t r -> p (t r)").bitcast(I32))
-        for quad in range(4):
-            nc.sync.dma_start(
-                key_bytes[32 * quad : 32 * quad + 4, :].bitcast(I32),
-                keys_scales[0, 4 * quad : 4 * quad + 4, :].bitcast(I32),
-            )
-        nc.sync.dma_start(rows[124:126, :], lam.rearrange("(j p) o -> j (p o)", p=P))
-        nc.sync.dma_start(rows[126:128, :], pull.rearrange("(j p) o -> j (p o)", p=P))
-        val_win = [tile([P, T], F32, "val_win%d" % j) for j in range(4)]
-        old_rows = [tile([P, M], F32, "old_rows%d" % j) for j in range(4)]
-        nc.sync.dma_start(val_win[0][:], vals[0:P, :])
-        nc.sync.dma_start(place_list[:], offs2)
-        for j in range(1, 4):
-            nc.sync.dma_start(val_win[j][:], vals[j * P : (j + 1) * P, :])
-        for j in range(4):
-            nc.sync.dma_start(old_rows[j][:], old[j * P : (j + 1) * P, :])
-
+        q_raw = tile([P, 4, Q], F32, "q_raw")
+        nc.sync.dma_start(q_raw[:], query.rearrange("(p j) q -> p j q", j=4))
         nc.vector.memset(steep_win[0:LAST, 0 : T - 1], 0.0)
         nc.vector.memset(steep_win[0:LAST, T - 1 : T], 0.0)
 
         ident = tile([P, P], F32, "ident")
         make_identity(nc, ident[:])
-        nc.gpsimd.memset(rows[0:112, :], 0.0)
         nc.gpsimd.memset(thr_win[0:LAST, :], 0.0)
         nc.gpsimd.memset(guess_win[0:LAST, :], 0.0)
+
+        warm = tile([P, 1], F32, "warm")
+        nc.scalar.activation(warm[:], ident[:, 0:1], ACT.Sigmoid)
 
         def gather_row(window, name, letter, after=None):
             got = tile([P, I], F32, name + "_got", after)
@@ -93,28 +81,35 @@ def tile_attend_answerodds_stepwise_written_kernel(
             nc.scalar.copy(col[:], turned[:, :, LAST])
             return col
 
+        def load_block(source, j, name, after):
+            block = tile([P, source.shape[1]], F32, "%s%d" % (name, j), after)
+            nc.sync.dma_start(block[:], source[j * P : (j + 1) * P, :])
+            return block
+
         steep_col = gather_row(steep_win, "steep", "A")
+        val_win = [load_block(vals, 0, "val_win", "steep_win")]
         thr_col = gather_row(thr_win, "thr", "B")
+        val_win.append(load_block(vals, 1, "val_win", "thr_win"))
+        rows = tile([P, P], F32, "rows", "steep_got")
+        nc.gpsimd.memset(rows[0:112, :], 0.0)
+        nc.sync.dma_start(rows[112:120, :], fade.rearrange("o (j p) -> (o j) p", p=P))
+        nc.sync.dma_start(rows[120:124, :], slot_gain.rearrange("o (j p) -> (o j) p", p=P))
+        nc.sync.dma_start(rows[124:126, :], lam.rearrange("(j p) o -> j (p o)", p=P))
+        nc.sync.dma_start(rows[126:128, :], pull.rearrange("(j p) o -> j (p o)", p=P))
+        val_win.append(load_block(vals, 2, "val_win", "thr_got"))
 
         q_bf = tile([P, Q, 4], BF16, "q_bf")
         nc.scalar.copy(q_bf[:], q_raw[:].rearrange("p j q -> p q j"))
+        val_win.append(load_block(vals, 3, "val_win", "q_raw"))
         q_codes = tile([P, Q], U32, "q_codes")
         q_scales = tile([P, Q], U8, "q_scales")
-        got_bytes = tile([P, I], U8, "got_bytes")
-        nc.vector.tensor_copy(got_bytes[:], key_bytes[:].indirect(slot_list[:]))
-        nc.vector.quantize_mx(q_codes[:].bitcast(FP8X4), q_scales[:], q_bf[:].rearrange("p q j -> p (q j)"))
         got_words = tile([P, I], U32, "got_words")
         nc.vector.tensor_copy(got_words[:], key_words[:].bitcast(U32).indirect(slot_list[:]))
+        got_bytes = tile([P, I], U8, "got_bytes", "key_words")
+        nc.vector.tensor_copy(got_bytes[:], key_bytes[:].indirect(slot_list[:]))
+        nc.vector.quantize_mx(q_codes[:].bitcast(FP8X4), q_scales[:], q_bf[:].rearrange("p q j -> p (q j)"))
         sig_bias = tile([P, 4], F32, "sig_bias")
         nc.vector.scalar_tensor_tensor(sig_bias[:], thr_col[:], -1.0, steep_col[:], ALU.mult, ALU.mult)
-
-        rows_turned = bank("B", [P, P], "rows_turned")
-        nc.tensor.transpose(rows_turned[:], rows[:], ident[:])
-        cols = tile([P, 16], F32, "cols")
-        nc.scalar.copy(cols[:], rows_turned[:, 112:128])
-        gain_all = bank("H", [P, 4, P], "gain_all")
-        for t in range(4):
-            nc.tensor.transpose(gain_all[:, t, :], cols[:, 8 + t : 9 + t].to_broadcast([P, P]), ident[:])
 
         score = [bank("DE"[h], [P, 2, Q], "score%d" % h) for h in range(2)]
         sig = tile([P, 4, Q], F32, "sig")
@@ -134,16 +129,14 @@ def tile_attend_answerodds_stepwise_written_kernel(
                 bias=sig_bias[:, t : t + 1], scale=steep_col[:, t : t + 1],
             )
 
-        guess_col = gather_row(guess_win, "guess", "C", "key_words")
+        guess_col = gather_row(guess_win, "guess", "C", "q_bf")
         miss_col = tile([P, 4], F32, "miss_col")
         nc.scalar.activation(miss_col[:], guess_col[:], ACT.Copy, scale=-1.0, bias=1.0)
 
-        places = [tile([P, M], F32, "places%d" % j, ["q_bf", "thr_col", "got_words", "q_codes"][j]) for j in range(4)]
+        old_rows = [load_block(old, j, "old_rows", ["key_words", "q_scales", "guess_win", "q_bf"][j]) for j in range(4)]
+        places = [tile([P, M], F32, "places%d" % j, ["thr_col", "got_words", "q_codes", "sig_bias"][j]) for j in range(4)]
         for j in range(4):
             nc.gpsimd.memset(places[j][:], 0.0)
-        negated = tile([P, 4], F32, "negated", "sig_bias")
-        nc.vector.tensor_scalar(negated[:], cols[:, 12:16], -1.0, None, ALU.mult)
-        neg_lam, neg_pull = negated[:, 0:2], negated[:, 2:4]
         prob = [tile([P, PAD + I], F32, "prob%d" % h) for h in range(2)]
         for h in range(2):
             nc.gpsimd.memset(prob[h][:, PAD - 1 : PAD], 0.0)
@@ -177,25 +170,34 @@ def tile_attend_answerodds_stepwise_written_kernel(
         for h in range(2):
             for t in range(4):
                 nc.tensor.transpose(log_turned[h][:, t, :], logc[:, t, h * P : (h + 1) * P], ident[:])
-        neg_s = [tile([P, I], F32, "neg_s%d" % h, ["val_win2", None][h]) for h in range(2)]
+        rows_turned = bank("E", [P, P], "rows_turned")
+        nc.tensor.transpose(rows_turned[:], rows[:], ident[:])
+        cols = tile([P, 16], F32, "cols", "miss_col")
+        nc.scalar.copy(cols[:], rows_turned[:, 112:128])
+        negated = tile([P, 4], F32, "negated")
+        nc.vector.tensor_scalar(negated[:], cols[:, 12:16], -1.0, None, ALU.mult)
+        neg_lam, neg_pull = negated[:, 0:2], negated[:, 2:4]
+        gain_all = bank("H", [P, 4, P], "gain_all")
+        for t in range(4):
+            nc.tensor.transpose(gain_all[:, t, :], cols[:, 8 + t : 9 + t].to_broadcast([P, P]), ident[:])
+        neg_s = [tile([P, I], F32, "neg_s%d" % h, ["thr_got", None][h]) for h in range(2)]
         neg_max = [tile([P, 1], F32, "neg_max%d" % h) for h in range(2)]
         for h in range(2):
             nc.vector.tensor_scalar(
                 neg_s[h][:], log_turned[h][:].rearrange("p t c -> p (t c)"), neg_lam[:, h : h + 1], None,
                 ALU.mult, ALU.min, accum_out=neg_max[h][:],
             )
-        gather_values(3, "D", "logc")
         total = [tile([P, 1], F32, "total%d" % h) for h in range(2)]
         for h in range(2):
             nc.scalar.activation(
                 prob[h][:, PAD:], neg_s[h][:], ACT.Exp, bias=neg_max[h][:], scale=-1.0, accum_out=total[h][:]
             )
-        v_bf = tile([P, 4, P, 4], BF16, "v_bf", "neg_s1")
-        for j in range(4):
-            nc.scalar.copy(v_bf[:, j, :, :].bitcast(F32), v_turned[j])
+        v_bf = [tile([P, 2, P, 4], BF16, "v_bf%d" % n, ["neg_s1", "neg_max1"][n]) for n in range(2)]
+        for j in range(3):
+            nc.scalar.copy(v_bf[j // 2][:, j % 2, :, :].bitcast(F32), v_turned[j])
         w_bf = []
         for h in range(2):
-            step = tile([P, I], F32, "step%d" % h, ["val_win3", "logc"][h])
+            step = tile([P, I], F32, "step%d" % h)
             nc.vector.scalar_tensor_tensor(
                 step[:], prob[h][:, PAD - 1 : PAD - 1 + I], neg_pull[:, h : h + 1], prob[h][:, PAD:],
                 ALU.mult, ALU.add,
@@ -210,7 +212,8 @@ def tile_attend_answerodds_stepwise_written_kernel(
             nc.scalar.copy(grouped[:].bitcast(F32), turn_pairs(weight[:], "FG"[h], "w_turned%d" % h))
             w_bf.append(grouped)
 
-        nc.vector.quantize_mx(v_codes[:].bitcast(FP8X4), v_scales[:], v_bf[:].rearrange("p j c t -> p (j c t)"))
+        gather_values(3, "D", "step1")
+        nc.scalar.copy(v_bf[1][:, 1, :, :].bitcast(F32), v_turned[3])
         w_codes = tile([P, Q], U32, "w_codes")
         w_scales = tile([P, Q], U8, "w_scales")
         for h in range(2):
@@ -218,6 +221,12 @@ def tile_attend_answerodds_stepwise_written_kernel(
                 w_codes[:, h * P : (h + 1) * P].bitcast(FP8X4),
                 w_scales[:, h * P : (h + 1) * P],
                 w_bf[h][:].rearrange("p c t -> p (c t)"),
+            )
+        for n in range(2):
+            nc.vector.quantize_mx(
+                v_codes[:, n * 2 * P : (n + 1) * 2 * P].bitcast(FP8X4),
+                v_scales[:, n * 2 * P : (n + 1) * 2 * P],
+                v_bf[n][:].rearrange("p j c t -> p (j c t)"),
             )
 
         for j in range(4):

from contextlib import ExitStack

import concourse.mybir as mybir
from concourse.masks import make_identity

D, T, I, Q, E, M = 512, 2048, 512, 256, 512, 1024
FLOPS = 2 * D * Q * I + 2 * I * E * Q
BYTES = 4 * D * Q + D * T + 16 * T + 3 * 4 * T + 4 * (2 * Q + I + M) + 4 * E * T + 2 * 4 * E * M + 2 * 128 * (I + Q) // 16

F32 = mybir.dt.float32
BF16 = mybir.dt.bfloat16
I32 = mybir.dt.int32
U32 = mybir.dt.uint32
U16 = mybir.dt.uint16
U8 = mybir.dt.uint8
FP8X4 = mybir.dt.float8_e4m3fn_x4
ALU = mybir.AluOpType
ACT = mybir.ActivationFunctionType

P = 128
LAST = P - 1
PAD = 8
HALF = M // 2


def tile_attend_answerodds_stepwise_written_kernel(
    tc, query, keys_words, keys_scales, guess, steep, thr, lam, pull, slot_gain, vals, old, fade, offs, offs2, out
):
    nc = tc.nc
    with ExitStack() as ctx:
        lists = ctx.enter_context(tc.tile_pool(name="lists", bufs=1))
        sb = ctx.enter_context(tc.tile_pool(name="sb", bufs=1))
        ps = ctx.enter_context(tc.psum_pool(name="ps", bufs=1))

        def bank(letter, shape, name):
            return ps.tile(shape, F32, name=name, tag="bank" + letter)

        def tile(shape, dtype, name, after=None):
            return sb.tile(shape, dtype, name=name, tag=after or name, align_bytes=64)

        slot_list = lists.tile([P, I // 16], U16, name="slot_list")
        place_list = lists.tile([P, Q // 16], U16, name="place_list")

        key_bytes = tile([P, T], U8, "key_bytes")
        nc.gpsimd.memset(key_bytes[:].bitcast(I32), 0)
        nc.sync.dma_start(slot_list[:], offs)
        for quad in range(4):
            nc.scalar.dma_start(
                key_bytes[32 * quad : 32 * quad + 4, :].bitcast(I32),
                keys_scales[0, 4 * quad : 4 * quad + 4, :].bitcast(I32),
            )
        steep_win = tile([P, T], F32, "steep_win")
        thr_win = tile([P, T], F32, "thr_win")
        guess_win = tile([P, T], F32, "guess_win")
        nc.sync.dma_start(steep_win[LAST:P, :], steep[0:1, :])
        nc.sync.dma_start(thr_win[LAST:P, :], thr[0:1, :])
        nc.sync.dma_start(guess_win[LAST:P, :], guess[0:1, :])
        nc.sync.dma_start(place_list[:], offs2)
        key_words = tile([P, T], I32, "key_words")
        nc.sync.dma_start(key_words[:], keys_words[0].rearrange("p t r -> p (t r)").bitcast(I32))
        q_raw = tile([P, 4, Q], F32, "q_raw")
        nc.sync.dma_start(q_raw[:], query.rearrange("(p j) q -> p j q", j=4))
        nc.vector.memset(steep_win[0:LAST, 0 : T - 1], 0.0)
        nc.vector.memset(steep_win[0:LAST, T - 1 : T], 0.0)

        ident = tile([P, P], F32, "ident")
        make_identity(nc, ident[:])
        nc.gpsimd.memset(thr_win[0:LAST, :], 0.0)
        nc.gpsimd.memset(guess_win[0:LAST, :], 0.0)

        warm = tile([P, 1], F32, "warm")
        nc.scalar.activation(warm[:], ident[:, 0:1], ACT.Sigmoid)

        def gather_row(window, name, letter, after=None):
            got = tile([P, I], F32, name + "_got", after)
            nc.vector.tensor_copy(got[:], window[:].indirect(slot_list[:]))
            turned = bank(letter, [P, 4, P], name + "_turned")
            for t in range(4):
                nc.tensor.transpose(turned[:, t, :], got[:, t * P : (t + 1) * P], ident[:])
            col = tile([P, 4], F32, name + "_col")
            nc.scalar.copy(col[:], turned[:, :, LAST])
            return col

        def load_block(source, j, name, after):
            block = tile([P, source.shape[1]], F32, "%s%d" % (name, j), after)
            nc.sync.dma_start(block[:], source[j * P : (j + 1) * P, :])
            return block

        steep_col = gather_row(steep_win, "steep", "A")
        val_win = [load_block(vals, 0, "val_win", "steep_win")]
        thr_col = gather_row(thr_win, "thr", "B")
        val_win.append(load_block(vals, 1, "val_win", "thr_win"))
        rows = tile([P, P], F32, "rows", "steep_got")
        nc.gpsimd.memset(rows[0:112, :], 0.0)
        nc.sync.dma_start(rows[112:120, :], fade.rearrange("o (j p) -> (o j) p", p=P))
        nc.sync.dma_start(rows[120:124, :], slot_gain.rearrange("o (j p) -> (o j) p", p=P))
        nc.sync.dma_start(rows[124:126, :], lam.rearrange("(j p) o -> j (p o)", p=P))
        nc.sync.dma_start(rows[126:128, :], pull.rearrange("(j p) o -> j (p o)", p=P))
        val_win.append(load_block(vals, 2, "val_win", "thr_got"))

        q_bf = tile([P, Q, 4], BF16, "q_bf")
        nc.scalar.copy(q_bf[:], q_raw[:].rearrange("p j q -> p q j"))
        val_win.append(load_block(vals, 3, "val_win", "q_raw"))
        q_codes = tile([P, Q], U32, "q_codes")
        q_scales = tile([P, Q], U8, "q_scales")
        got_words = tile([P, I], U32, "got_words")
        nc.vector.tensor_copy(got_words[:], key_words[:].bitcast(U32).indirect(slot_list[:]))
        got_bytes = tile([P, I], U8, "got_bytes", "key_words")
        nc.vector.tensor_copy(got_bytes[:], key_bytes[:].indirect(slot_list[:]))
        nc.vector.quantize_mx(q_codes[:].bitcast(FP8X4), q_scales[:], q_bf[:].rearrange("p q j -> p (q j)"))
        sig_bias = tile([P, 4], F32, "sig_bias")
        nc.vector.scalar_tensor_tensor(sig_bias[:], thr_col[:], -1.0, steep_col[:], ALU.mult, ALU.mult)

        score = [bank("DE"[h], [P, 2, Q], "score%d" % h) for h in range(2)]
        sig = tile([P, 4, Q], F32, "sig")
        for t in range(4):
            nc.tensor.matmul_mx(
                score[t // 2][:, t % 2, :],
                lhsT=got_words[:, t * P : (t + 1) * P].bitcast(FP8X4),
                lhsT_scale=got_bytes[:, t * P : (t + 1) * P],
                rhs=q_codes[:].bitcast(FP8X4),
                rhs_scale=q_scales[:],
                start=True,
                stop=True,
            )
        for t in range(4):
            nc.scalar.activation(
                sig[:, t, :], score[t // 2][:, t % 2, :], ACT.Sigmoid,
                bias=sig_bias[:, t : t + 1], scale=steep_col[:, t : t + 1],
            )

        guess_col = gather_row(guess_win, "guess", "C", "q_bf")
        miss_col = tile([P, 4], F32, "miss_col")
        nc.scalar.activation(miss_col[:], guess_col[:], ACT.Copy, scale=-1.0, bias=1.0)

        old_rows = [load_block(old, j, "old_rows", ["key_words", "q_scales", "guess_win", "q_bf"][j]) for j in range(4)]
        places = [tile([P, M], F32, "places%d" % j, ["thr_col", "got_words", "q_codes", "sig_bias"][j]) for j in range(4)]
        for j in range(4):
            nc.gpsimd.memset(places[j][:], 0.0)
        prob = [tile([P, PAD + I], F32, "prob%d" % h) for h in range(2)]
        for h in range(2):
            nc.gpsimd.memset(prob[h][:, PAD - 1 : PAD], 0.0)

        logc = tile([P, 4, Q], F32, "logc")
        for t in range(4):
            nc.scalar.activation(
                logc[:, t, :], sig[:, t, :], ACT.Ln, bias=guess_col[:, t : t + 1], scale=miss_col[:, t : t + 1]
            )

        v_turned = []
        v_codes = tile([P, E], U32, "v_codes")
        v_scales = tile([P, E], U8, "v_scales")

        def turn_pairs(src, letter, name):
            words = src.bitcast(F32)
            turned = bank(letter, [P, 2, P], name)
            for u in range(2):
                nc.tensor.transpose(turned[:, u, :], words[:, u : I // 2 : 2], ident[:])
            return turned[:].rearrange("p u c -> p c u")

        def gather_values(j, letter, after=None):
            got = tile([P, I], BF16, "val_got%d" % j, after)
            nc.vector.tensor_copy(got[:], val_win[j][:].indirect(slot_list[:]))
            v_turned.append(turn_pairs(got[:], letter, "val_turned%d" % j))

        for j in range(3):
            gather_values(j, "ABC"[j])

        log_turned = [bank("FG"[h], [P, 4, P], "log_turned%d" % h) for h in range(2)]
        for h in range(2):
            for t in range(4):
                nc.tensor.transpose(log_turned[h][:, t, :], logc[:, t, h * P : (h + 1) * P], ident[:])
        rows_turned = bank("E", [P, P], "rows_turned")
        nc.tensor.transpose(rows_turned[:], rows[:], ident[:])
        cols = tile([P, 16], F32, "cols", "miss_col")
        nc.scalar.copy(cols[:], rows_turned[:, 112:128])
        negated = tile([P, 4], F32, "negated")
        nc.vector.tensor_scalar(negated[:], cols[:, 12:16], -1.0, None, ALU.mult)
        neg_lam, neg_pull = negated[:, 0:2], negated[:, 2:4]
        gain_all = bank("H", [P, 4, P], "gain_all")
        for t in range(4):
            nc.tensor.transpose(gain_all[:, t, :], cols[:, 8 + t : 9 + t].to_broadcast([P, P]), ident[:])
        neg_s = [tile([P, I], F32, "neg_s%d" % h, ["thr_got", None][h]) for h in range(2)]
        neg_max = [tile([P, 1], F32, "neg_max%d" % h) for h in range(2)]
        for h in range(2):
            nc.vector.tensor_scalar(
                neg_s[h][:], log_turned[h][:].rearrange("p t c -> p (t c)"), neg_lam[:, h : h + 1], None,
                ALU.mult, ALU.min, accum_out=neg_max[h][:],
            )
        total = [tile([P, 1], F32, "total%d" % h) for h in range(2)]
        for h in range(2):
            nc.scalar.activation(
                prob[h][:, PAD:], neg_s[h][:], ACT.Exp, bias=neg_max[h][:], scale=-1.0, accum_out=total[h][:]
            )
        v_bf = [tile([P, 2, P, 4], BF16, "v_bf%d" % n, ["neg_s1", "neg_max1"][n]) for n in range(2)]
        for j in range(3):
            nc.scalar.copy(v_bf[j // 2][:, j % 2, :, :].bitcast(F32), v_turned[j])
        w_bf = []
        for h in range(2):
            step = tile([P, I], F32, "step%d" % h)
            nc.vector.scalar_tensor_tensor(
                step[:], prob[h][:, PAD - 1 : PAD - 1 + I], neg_pull[:, h : h + 1], prob[h][:, PAD:],
                ALU.mult, ALU.add,
            )
            inv = tile([P, 1], F32, "inv%d" % h)
            nc.vector.reciprocal(inv[:], total[h][:])
            weight = tile([P, I], BF16, "weight%d" % h)
            nc.vector.scalar_tensor_tensor(
                weight[:], step[:], inv[:], gain_all[:].rearrange("q t p -> q (t p)"), ALU.mult, ALU.mult
            )
            grouped = tile([P, P, 4], BF16, "w_bf%d" % h)
            nc.scalar.copy(grouped[:].bitcast(F32), turn_pairs(weight[:], "FG"[h], "w_turned%d" % h))
            w_bf.append(grouped)

        gather_values(3, "D", "step1")
        nc.scalar.copy(v_bf[1][:, 1, :, :].bitcast(F32), v_turned[3])
        w_codes = tile([P, Q], U32, "w_codes")
        w_scales = tile([P, Q], U8, "w_scales")
        for h in range(2):
            nc.vector.quantize_mx(
                w_codes[:, h * P : (h + 1) * P].bitcast(FP8X4),
                w_scales[:, h * P : (h + 1) * P],
                w_bf[h][:].rearrange("p c t -> p (c t)"),
            )
        for n in range(2):
            nc.vector.quantize_mx(
                v_codes[:, n * 2 * P : (n + 1) * 2 * P].bitcast(FP8X4),
                v_scales[:, n * 2 * P : (n + 1) * 2 * P],
                v_bf[n][:].rearrange("p j c t -> p (j c t)"),
            )

        for j in range(4):
            acc = bank("EABC"[j], [P, Q], "acc%d" % j)
            nc.tensor.matmul_mx(
                acc[:],
                lhsT=v_codes[:, j * P : (j + 1) * P].bitcast(FP8X4),
                lhsT_scale=v_scales[:, j * P : (j + 1) * P],
                rhs=w_codes[:].bitcast(FP8X4),
                rhs_scale=w_scales[:],
                start=True,
                stop=True,
            )
            mixed = tile([P, Q], F32, "mixed%d" % j)
            nc.scalar.copy(mixed[:], acc[:])
            nc.vector.tensor_copy(places[j][:].indirect(place_list[:]), mixed[:])

        faded = []
        for b in range(8):
            turned = bank("EABC"[b % 4], [P, 4, P], "old_turned%d" % b)
            for j in range(4):
                nc.tensor.transpose(turned[:, j, :], old_rows[j][:, b * P : (b + 1) * P], ident[:])
            scaled = tile([P, E], F32, "faded%d" % b)
            nc.scalar.activation(
                scaled[:], turned[:].rearrange("p j c -> p (j c)"), ACT.Copy, scale=cols[:, b : b + 1]
            )
            faded.append(scaled)
        for half in range(2):
            cut = slice(half * HALF, (half + 1) * HALF)
            for j in range(4):
                back = bank(["DFGH", "EABC"][half][j], [P, 4, P], "back%d_%d" % (j, half))
                for n in range(4):
                    nc.tensor.transpose(back[:, n, :], faded[4 * half + n][:, j * P : (j + 1) * P], ident[:])
                result = tile([P, HALF], F32, "result%d_%d" % (j, half))
                nc.vector.tensor_tensor(result[:], back[:].rearrange("p n c -> p (n c)"), places[j][:, cut], ALU.add)
                nc.sync.dma_start(out[j * P : (j + 1) * P, cut], result[:])
